import numpy as np
import ml_dtypes


def mxq(x, axis, fmt="e4m3"):
    dtype, down = {"e4m3": (ml_dtypes.float8_e4m3fn, 7), "e5m2": (ml_dtypes.float8_e5m2, 14)}[fmt]
    v = np.moveaxis(np.asarray(x, np.float32).astype(ml_dtypes.bfloat16).astype(np.float64), axis, -1)
    blocks = v.reshape(v.shape[:-1] + (-1, 32))
    amax = np.abs(blocks).max(-1, keepdims=True)
    byte = np.maximum(np.where(amax > 0, np.frexp(amax)[1] - 1 + 127, 0) - down, 1)
    scale = np.exp2(byte - 127.0)
    codes = (blocks / scale).astype(np.float32).astype(dtype).astype(np.float64)
    return np.moveaxis((codes * scale).reshape(v.shape), -1, axis)


WIDE = False


def mx_kscale(k):
    if not WIDE:
        return np.ones(k)
    levels = np.array([10, -10, 5, -5, 0])
    if k % 512:
        return np.exp2(np.random.permutation(np.resize(levels, k // 32))).repeat(32)
    a = np.empty((k // 512, 16))
    for p in range(k // 512):
        a[p, :8] = np.random.permutation(np.resize(levels, 8))
        for g in range(8):
            far = levels[np.abs(levels - a[p, g]) >= 10]
            a[p, g + 8] = far[np.random.randint(len(far))]
    return np.exp2(a.ravel()).repeat(32)


BF16 = ml_dtypes.bfloat16


def bf(x):
    return np.asarray(x, np.float32).astype(BF16)


def f64(x):
    return np.asarray(x).astype(np.float64)


E2M1 = np.array([0.0, 0.5, 1.0, 1.5, 2.0, 3.0, 4.0, 6.0, -0.0, -0.5, -1.0, -1.5, -2.0, -3.0, -4.0, -6.0])


def pack_weight(w, fmt):
    k, n = w.shape
    w = f64(bf(w)).reshape(k // 32, 32, n)
    amax = np.abs(w).max(1)
    if fmt == "e4m3":
        byte = np.frexp(amax)[1] - 1 + 127 - 7
    else:
        mant, ex = np.frexp(amax / 6.0)
        byte = np.where(mant > 0.5, ex, ex - 1) + 127
    byte = np.clip(np.where(amax > 0, byte, 1), 1, 254)
    scaled = (w * np.exp2(127.0 - byte)[:, None, :]).reshape(k, n).astype(np.float32)
    by_word = np.ascontiguousarray(scaled.reshape(k // 512, 128, 4, n).transpose(0, 1, 3, 2))
    if fmt == "e4m3":
        words = by_word.astype(ml_dtypes.float8_e4m3fn).view(np.uint8)
    else:
        c = by_word.astype(ml_dtypes.float4_e2m1fn).view(np.uint8) & 0xF
        words = c[..., 0::2] | (c[..., 1::2] << 4)
    return np.ascontiguousarray(words), np.ascontiguousarray(byte.astype(np.uint8).reshape(k // 512, 16, n))


def unpack_weight(words, scales, fmt):
    g, p, n, _ = words.shape
    if fmt == "e4m3":
        vals = np.ascontiguousarray(words).view(ml_dtypes.float8_e4m3fn).astype(np.float64)
    else:
        nib = np.empty((g, p, n, 4), np.uint8)
        nib[..., 0::2] = words & 0xF
        nib[..., 1::2] = words >> 4
        vals = E2M1[nib]
    vals = vals * np.repeat(np.exp2(scales.astype(np.float64) - 127.0), 8, axis=1)[..., None]
    return vals.transpose(0, 1, 3, 2).reshape(g * 512, n)
def pack4(w):
    words, scales = pack_weight(w, "e2m1")
    return words.reshape(words.shape[0], 128, -1), scales


def unpack4(words, scales):
    return unpack_weight(words.reshape(words.shape[0], 128, -1, 2), scales, "e2m1")


E4M3FN = np.array([(-1.0 if i & 128 else 1.0) * ((1.0 + (i & 7) / 8.0) * 2.0 ** (((i >> 3) & 15) - 7) if i & 120 else (i & 7) * 2.0 ** -9) for i in range(256)])


def e4m3fn_bytes(y):
    return np.clip(np.asarray(y, np.float64), -448.0, 448.0).astype(np.float32).astype(ml_dtypes.float8_e4m3fn).view(np.uint8)


def e4m3fn_values(b):
    return E4M3FN[b]


T, D, V, B = 512, 2048, 1536, 128


def setup_inputs():
    s, t = mx_kscale(D), mx_kscale(D)
    states = np.random.standard_normal((T, D))
    X = states * s
    W = 2 * np.random.standard_normal((D, D)) / np.sqrt(D) / s
    P = np.random.standard_normal((D, V)) / np.sqrt(D) / t[:, None]
    X_scale = (np.abs(X).reshape(T, D // B, B).max(axis=2) / 448).astype(np.float32)
    W_scale = (np.abs(W).reshape(D // B, B, D // B, B).max(axis=(1, 3)) / 448).astype(np.float32)
    X_bytes = e4m3fn_bytes(X / np.repeat(f64(X_scale), B, axis=1))
    W_bytes = e4m3fn_bytes(W / np.repeat(np.repeat(f64(W_scale), B, axis=0), B, axis=1))
    P_words, P_scales = pack4(P)
    return {"X_bytes": X_bytes, "X_scale": X_scale,
            "W_bytes": W_bytes, "W_scale": W_scale,
            "resid": bf(states),
            "gain": bf((1 + 0.1 * np.random.standard_normal(D)) * t),
            "P_words": P_words, "P_scales": P_scales}


def reference(X_bytes, X_scale, W_bytes, W_scale, resid, gain, P_words, P_scales):
    X = e4m3fn_values(X_bytes) * np.repeat(f64(X_scale), B, axis=1)
    W = e4m3fn_values(W_bytes) * np.repeat(np.repeat(f64(W_scale), B, axis=0), B, axis=1)
    z = mxq(X, 1, "e4m3") @ mxq(W, 1, "e4m3").T
    h = (z / (1 + np.exp(-z)) + f64(resid)) * f64(gain)
    return mxq(h, 1, "e4m3") @ unpack4(P_words, P_scales)

@@ -1,0 +1,416 @@
+from contextlib import ExitStack
+
+import concourse.mybir as mybir
+from concourse.masks import make_identity
+
+T, D, V = 512, 2048, 1536
+P = 128
+FLOPS = 2 * T * D * (D + V)
+
+F32 = mybir.dt.float32
+BF16 = mybir.dt.bfloat16
+U32 = mybir.dt.uint32
+I32 = mybir.dt.int32
+U8 = mybir.dt.uint8
+FP8 = mybir.dt.float8_e4m3fn
+FP8X4 = mybir.dt.float8_e4m3fn_x4
+FP4X4 = mybir.dt.float4_e2m1fn_x4
+COPY = mybir.ActivationFunctionType.Copy
+SILU = mybir.ActivationFunctionType.Silu
+MULT = mybir.AluOpType.mult
+ADD = mybir.AluOpType.add
+
+NB = 4
+NG = 4
+NC = 4
+NT = 4
+NV = 3
+
+X_ON_SCALAR = (3,)
+MODES = {}
+DEFAULT = "bbbc"
+HADD = {}
+HDEF = "v"
+
+
+def tile_fp8_extra_decoding_head_d4_kernel(
+    tc, X_bytes, X_scale, W_bytes, W_scale, resid, gain, P_words, P_scales, out
+):
+    nc = tc.nc
+    with ExitStack() as ctx:
+        keep = ctx.enter_context(tc.tile_pool(name="keep", bufs=1))
+        work = ctx.enter_context(tc.tile_pool(name="work", bufs=3))
+        psum = ctx.enter_context(tc.psum_pool(name="psum", bufs=4))
+
+        xs = keep.tile([P, NT, D // P], F32, name="xs")
+        xb = [keep.tile([P, NT, 1024], U8, name="xb%d" % h, align_bytes=64) for h in range(2)]
+        wb = [keep.tile([P, NG, NB, 512], U8, name="wb%d" % c, align_bytes=64) for c in range(NC)]
+        wsc = keep.tile([P, 256], F32, name="wsc")
+        ks = keep.tile([P, 16, NG], F32, name="ks")
+        gt = keep.tile([P, NC, 4], BF16, name="gt")
+        rt = [keep.tile([P, NT, 512], BF16, name="rt%d" % c, align_bytes=64) for c in range(NC)]
+        pw = keep.tile([P, NG, 2 * V], U8, name="pw", align_bytes=64)
+        psc = keep.tile([P, NG, V], U8, name="psc", align_bytes=64)
+        ident = keep.tile([P, P], F32, name="ident")
+        warm = keep.tile([P, 1], F32, name="warm")
+
+        nc.gpsimd.memset(warm[:], 0.0)
+        nc.scalar.activation(warm[:], warm[:], SILU)
+        make_identity(nc, ident[:])
+        identb = keep.tile([P, P], BF16, name="identb")
+        nc.vector.tensor_copy(out=identb[:], in_=ident[:])
+        nc.gpsimd.memset(psc[:].rearrange("p g n -> p (g n)").bitcast(I32), 0)
+
+        nc.sync.dma_start(out=xs[:], in_=X_scale.rearrange("(a p) j -> p a j", p=P))
+
+        def load_x(h):
+            nc.sync.dma_start(
+                out=xb[h][:],
+                in_=X_bytes[:, 1024 * h : 1024 * (h + 1)].rearrange("(a p) k -> p a k", p=P),
+            )
+
+        def load_w(c, g0, g1):
+            for g in range(g0, g1):
+                nc.sync.dma_start(
+                    out=wb[c][:, g, :, :],
+                    in_=W_bytes[512 * c : 512 * (c + 1), 512 * g : 512 * (g + 1)].rearrange("(a p) k -> p a k", p=P),
+                )
+
+        def load_r(c):
+            nc.sync.dma_start(
+                out=rt[c][:],
+                in_=resid[:, 512 * c : 512 * (c + 1)].rearrange("(a p) k -> p a k", p=P),
+            )
+
+        nc.scalar.dma_start(out=wsc[:], in_=W_scale.rearrange("i j -> (i j)").partition_broadcast(P))
+        nc.scalar.dma_start(out=gt[:], in_=gain.rearrange("(c p t) -> p c t", p=P, t=4))
+        load_x(0)
+        load_w(0, 0, 2)
+        load_x(1)
+        load_w(0, 2, 4)
+        load_w(1, 0, 4)
+        load_r(0)
+        load_w(2, 0, 4)
+        load_r(1)
+        load_w(3, 0, 4)
+        for q in range(4):
+            nc.sync.dma_start(
+                out=psc[32 * q : 32 * q + 4, :, :].rearrange("p g n -> p (g n)").bitcast(I32).rearrange("p (g n) -> p g n", g=NG),
+                in_=P_scales[:, 4 * q : 4 * q + 4, :].bitcast(I32).rearrange("g r n -> r g n"),
+            )
+        nc.sync.dma_start(out=pw[:], in_=P_words.rearrange("g p n -> p g n"))
+        load_r(2)
+        load_r(3)
+
+        for q in range(4):
+            rows = slice(32 * q, 32 * q + 32)
+            nc.vector.tensor_copy(
+                out=ks[rows, :, :],
+                in_=wsc[rows, :].rearrange("p (i g r) -> p i g r", i=16, g=NG)[:, :, :, q],
+            )
+
+        xc = [keep.tile([P, 512], U32, name="xc%d" % g, align_bytes=64) for g in range(NG)]
+        xp = [keep.tile([P, 512], U8, name="xp%d" % g, align_bytes=64) for g in range(NG)]
+        hc = [keep.tile([P, 512], U32, name="hc%d" % c, align_bytes=64) for c in range(NC)]
+        hp = [keep.tile([P, 512], U8, name="hp%d" % c, align_bytes=64) for c in range(NC)]
+
+        units = []
+        for g in range(NG):
+            units.append(("x", 0, g))
+            units.append(("w", 0, g))
+        for c in range(1, NC):
+            for g in range(NG):
+                units.append(("w", c, g))
+        n_units = len(units)
+        wide, bank, grp, codes, planes = {}, {}, {}, {}, {}
+        z, s_t, u_t, hb, hg = {}, {}, {}, {}, {}
+
+        def mode(c, g):
+            return MODES.get((c, g), DEFAULT)
+
+        def permuted(i, a):
+            kind, c, g = units[i]
+            if kind == "x":
+                return a not in X_ON_SCALAR
+            return mode(c, g)[a] == "a"
+
+        def widen(i):
+            kind, c, g = units[i]
+            w = work.tile([P, NB, 512], BF16, name="wide", align_bytes=64, bufs=4)
+            wide[i] = w
+            if kind == "w":
+                m = mode(c, g)
+                n_a = m.count("a")
+                assert m[:n_a] == "a" * n_a
+                if n_a < NB:
+                    nc.scalar.copy(
+                        w[:, n_a:, :].rearrange("p a k -> p (a k)"),
+                        wb[c][:, g, n_a:, :].rearrange("p a k -> p (a k)").bitcast(FP8),
+                    )
+                for a in range(n_a):
+                    for q in range(4):
+                        k0 = 16 * (4 * c + a) + 4 * g + q
+                        nc.vector.tensor_scalar(
+                            out=w[:, a, :].rearrange("p (u j e) -> p j u e", u=2, e=2)[:, 32 * q : 32 * q + 32, :, :],
+                            in0=wb[c][:, g, a, P * q : P * (q + 1)].bitcast(FP8).rearrange("p (j u e) -> p j u e", u=2, e=2),
+                            scalar1=wsc[:, k0 : k0 + 1], scalar2=None, op0=MULT,
+                        )
+                return
+            h, off = g // 2, 512 * (g % 2)
+            for a in range(NT):
+                for q in range(4):
+                    src = xb[h][:, a, off + P * q : off + P * (q + 1)].bitcast(FP8)
+                    scale = xs[:, a, 4 * g + q : 4 * g + q + 1]
+                    if permuted(i, a):
+                        dst = w[:, a, :].rearrange("p (u j e) -> p j u e", u=2, e=2)[:, 32 * q : 32 * q + 32, :, :]
+                        nc.vector.tensor_scalar(
+                            out=dst,
+                            in0=src.rearrange("p (j u e) -> p j u e", u=2, e=2),
+                            scalar1=scale, scalar2=None, op0=MULT,
+                        )
+                    else:
+                        nc.scalar.activation(w[:, a, P * q : P * (q + 1)], src, COPY, scale=scale)
+
+        def trans(i, b):
+            kind, c, g = units[i]
+            bk = psum.tile([P, 512], F32, name="t", bufs=4)
+            bank[i, b] = bk
+            dst = bk[:].rearrange("p (a u n) -> p a u n", a=2, u=2)
+            words = wide[i][:].rearrange("p a k -> p (a k)").bitcast(F32)
+            for al in range(2):
+                a = 2 * b + al
+                for u in range(2):
+                    if permuted(i, a):
+                        src = words[:, 256 * a + 128 * u : 256 * a + 128 * (u + 1)]
+                    else:
+                        src = words[:, 256 * a + u : 256 * (a + 1) : 2]
+                    nc.tensor.transpose(dst[:, al, u, :], src, ident[:])
+
+        def evac(i, b):
+            kind, c, g = units[i]
+            if b == 0:
+                grp[i] = work.tile([P, 2048], BF16, name="grp", align_bytes=64, bufs=3)
+            bk = bank.pop((i, b))
+            if kind == "x":
+                dst = grp[i][:, 1024 * b : 1024 * (b + 1)].bitcast(F32).rearrange("p (a n u) -> p a n u", a=2, u=2)
+                src = bk[:].rearrange("p (a u n) -> p a n u", a=2, u=2)
+                if b == 0:
+                    nc.vector.tensor_copy(out=dst, in_=src)
+                else:
+                    nc.scalar.copy(dst, src)
+                return
+            m = mode(c, g)
+            if m[2 * b : 2 * b + 2] in ("aa", "AA"):
+                dst = grp[i][:, 1024 * b : 1024 * (b + 1)].bitcast(F32).rearrange("p (a n u) -> p a n u", a=2, u=2)
+                nc.scalar.copy(dst, bk[:].rearrange("p (a u n) -> p a n u", a=2, u=2))
+                return
+            for al in range(2):
+                a = 2 * b + al
+                if m[a] == "a":
+                    dst = grp[i][:, 512 * a : 512 * (a + 1)].bitcast(F32).rearrange("p (n u) -> p n u", u=2)
+                    nc.scalar.copy(dst, bk[:, 256 * al : 256 * (al + 1)].rearrange("p (u n) -> p n u", u=2))
+                    continue
+                dst = grp[i][:, 512 * a : 512 * (a + 1)].rearrange("p (n u e) -> p n u e", u=2, e=2)
+                src = bk[:, 256 * al : 256 * (al + 1)].bitcast(BF16).rearrange("p (u n e) -> p n u e", u=2, e=2)
+                scale = ks[:, 4 * c + a, g : g + 1]
+                if m[a] == "c":
+                    nc.scalar.activation(dst, src, COPY, scale=scale)
+                else:
+                    nc.vector.tensor_scalar(out=dst, in0=src, scalar1=scale, scalar2=None, op0=MULT)
+
+        def quant(i):
+            kind, c, g = units[i]
+            if kind == "x":
+                cd, pl = xc[g], xp[g]
+            else:
+                cd = work.tile([P, 512], U32, name="wcodes", align_bytes=64, bufs=3)
+                pl = work.tile([P, 512], U8, name="wplane", align_bytes=64, bufs=3)
+            codes[i], planes[i] = cd, pl
+            nc.vector.quantize_mx(out=cd[:].bitcast(FP8X4), scales=pl[:], in_=grp.pop(i)[:])
+
+        def mm(i):
+            kind, c, g = units[i]
+            if kind == "x":
+                return
+            for a in range(NT):
+                if g == 0:
+                    z[c, a] = psum.tile([P, 512], F32, name="z", bufs=4)
+                cols = slice(P * a, P * (a + 1))
+                nc.tensor.matmul_mx(
+                    out=z[c, a][:],
+                    lhsT=xc[g][:, cols].bitcast(FP8X4), lhsT_scale=xp[g][:, cols],
+                    rhs=codes[i][:].bitcast(FP8X4), rhs_scale=planes[i][:],
+                    start=(g == 0), stop=(g == NG - 1),
+                )
+
+        def silu(c, a):
+            s = work.tile([P, 4, P], F32, name="s", bufs=6)
+            s_t[c, a] = s
+            nc.scalar.activation(s[:], z.pop((c, a))[:].rearrange("p (m t) -> p t m", t=4), SILU)
+
+        def hadd(c, a):
+            if HADD.get((c, a), HDEF) == "p":
+                return
+            u = work.tile([P, 4, P], F32, name="u", bufs=3)
+            u_t[c, a] = u
+            nc.vector.tensor_tensor(
+                out=u[:], in0=s_t.pop((c, a))[:],
+                in1=rt[c][:, a, :].rearrange("p (m t) -> p t m", t=4), op=ADD,
+            )
+
+        def htrans(c, a):
+            bk = psum.tile([P, 512], F32, name="t", bufs=4)
+            hb[c, a] = bk
+            if HADD.get((c, a), HDEF) == "p":
+                s = s_t.pop((c, a))
+                for t in range(4):
+                    o = bk[:, P * t : P * (t + 1)]
+                    nc.tensor.matmul(o, lhsT=rt[c][:, a, t : 512 : 4], rhs=identb[:], start=True, stop=False)
+                    nc.tensor.matmul(o, lhsT=s[:, t, :], rhs=ident[:], start=False, stop=True, is_transpose=True)
+                return
+            u = u_t.pop((c, a))
+            for t in range(4):
+                nc.tensor.transpose(bk[:, P * t : P * (t + 1)], u[:, t, :], ident[:])
+
+        def hevac(c, a):
+            h = work.tile([P, P, 4], BF16, name="hg", align_bytes=64, bufs=3)
+            hg[c, a] = h
+            nc.vector.tensor_tensor(
+                out=h[:], in0=hb.pop((c, a))[:].rearrange("p (t n) -> p n t", t=4),
+                in1=gt[:, c, :].unsqueeze(1).to_broadcast([P, P, 4]), op=MULT,
+            )
+
+        def hquant(c, a):
+            cols = slice(P * a, P * (a + 1))
+            nc.vector.quantize_mx(
+                out=hc[c][:, cols].bitcast(FP8X4), scales=hp[c][:, cols],
+                in_=hg.pop((c, a))[:].rearrange("p n t -> p (n t)"),
+            )
+
+        acc = {}
+
+        def logits(a, v, cs):
+            for c in cs:
+                cols = slice(P * a, P * (a + 1))
+                nc.tensor.matmul_mx(
+                    out=acc[a, v][:],
+                    lhsT=hc[c][:, cols].bitcast(FP8X4), lhsT_scale=hp[c][:, cols],
+                    rhs=pw[:, c, 1024 * v : 1024 * (v + 1)].bitcast(FP4X4),
+                    rhs_scale=psc[:, c, 512 * v : 512 * (v + 1)],
+                    start=(c == 0), stop=(c == NC - 1),
+                )
+
+        def store(a, v):
+            o = work.tile([P, 512], F32, name="o", bufs=6)
+            if (a * NV + v) % 2:
+                nc.scalar.copy(o[:], acc.pop((a, v))[:])
+            else:
+                nc.vector.tensor_copy(out=o[:], in_=acc.pop((a, v))[:])
+            nc.sync.dma_start(out=out[P * a : P * (a + 1), 512 * v : 512 * (v + 1)], in_=o[:])
+
+        ready = []
+        hq = None
+        with tc.manual_schedule():
+            widen(0)
+            widen(1)
+            for s in range(1, n_units + 3):
+                if s + 1 < n_units:
+                    widen(s + 1)
+                it = s - 1
+                iq = s - 2
+                im = s - 3
+                h = ready.pop(0) if ready else None
+                if h:
+                    hadd(*h)
+                if 0 <= iq < n_units:
+                    quant(iq)
+                if hq:
+                    hquant(*hq)
+                if it < n_units:
+                    trans(it, 0)
+                    evac(it, 0)
+                if h:
+                    htrans(*h)
+                    hevac(*h)
+                if it < n_units:
+                    trans(it, 1)
+                    evac(it, 1)
+                hq = h
+                if im >= 0:
+                    mm(im)
+                    kind, c, g = units[im]
+                    if kind == "w" and g == NG - 1:
+                        for a in range(NT):
+                            silu(c, a)
+                            ready.append((c, a))
+            last = NC - 1
+
+            def open_group(a, v, tag, cs):
+                if tag == "t":
+                    acc[a, v] = psum.tile([P, 512], F32, name="t", bufs=4)
+                else:
+                    acc[a, v] = psum.tile([P, 512], F32, name="z", bufs=4)
+                logits(a, v, cs)
+
+            early = range(NC - 1)
+            every = range(NC)
+            hquant(*hq)
+            hadd(last, 0)
+            hadd(last, 1)
+            for v in range(NV):
+                open_group(0, v, "t", early)
+            htrans(last, 0)
+            hevac(last, 0)
+            hadd(last, 2)
+            hquant(last, 0)
+            for v in range(NV):
+                open_group(1, v, "z", early)
+            htrans(last, 1)
+            hevac(last, 1)
+            hadd(last, 3)
+            hquant(last, 1)
+            for v in range(NV):
+                logits(0, v, [last])
+                store(0, v)
+            htrans(last, 2)
+            hevac(last, 2)
+            for v in range(NV):
+                logits(1, v, [last])
+                store(1, v)
+            hquant(last, 2)
+            htrans(last, 3)
+            hevac(last, 3)
+            for v in range(NV):
+                open_group(2, v, "t" if v < 2 else "z", every)
+                if v == 0:
+                    hquant(last, 3)
+                store(2, v)
+            for v in range(NV - 1):
+                open_group(3, v, "z" if v == 0 else "t", every)
+                store(3, v)
+            v = NV - 1
+            a = NT - 1
+            cols = slice(P * a, P * (a + 1))
+            for part, (q0, q1) in enumerate(((0, 3), (3, 4))):
+                if part:
+                    bk = psum.tile([P, 512], F32, name="z", bufs=4)
+                else:
+                    bk = psum.tile([P, 512], F32, name="t", bufs=4)
+                for q in range(q0, q1):
+                    n0 = 512 * v + P * q
+                    for c in every:
+                        nc.tensor.matmul_mx(
+                            out=bk[:, P * q : P * (q + 1)],
+                            lhsT=hc[c][:, cols].bitcast(FP8X4), lhsT_scale=hp[c][:, cols],
+                            rhs=pw[:, c, 2 * n0 : 2 * n0 + 2 * P].bitcast(FP4X4),
+                            rhs_scale=psc[:, c, n0 : n0 + P],
+                            start=(c == 0), stop=(c == NC - 1),
+                        )
+                width = P * (q1 - q0)
+                o = work.tile([P, 512], F32, name="oh", bufs=2)
+                if part:
+                    nc.vector.tensor_copy(out=o[:, :width], in_=bk[:, P * q0 : P * q1])
+                else:
+                    nc.scalar.copy(o[:, :width], bk[:, P * q0 : P * q1])
+                n0 = 512 * v + P * q0
+                nc.sync.dma_start(out=out[P * a : P * (a + 1), n0 : n0 + width], in_=o[:, :width])

@@ -28,9 +28,15 @@ NV = 3
 
 X_ON_SCALAR = (3,)
 MODES = {}
-DEFAULT = "bbbc"
+DEFAULT = "aaae"
 HADD = {}
 HDEF = "v"
+WB = 4
+LEAD = 1
+HP = "C"
+XEV = "ss"
+SIL = 4
+ORD = 0
 
 
 def tile_fp8_extra_decoding_head_d4_kernel(
@@ -57,6 +63,9 @@ def tile_fp8_extra_decoding_head_d4_kernel(
         nc.gpsimd.memset(warm[:], 0.0)
         nc.scalar.activation(warm[:], warm[:], SILU)
         make_identity(nc, ident[:])
+        if HP == "B":
+            gb = keep.tile([P, D], BF16, name="gb")
+            nc.scalar.dma_start(out=gb[:], in_=gain.partition_broadcast(P))
         identb = keep.tile([P, P], BF16, name="identb")
         nc.vector.tensor_copy(out=identb[:], in_=ident[:])
         nc.gpsimd.memset(psc[:].rearrange("p g n -> p (g n)").bitcast(I32), 0)
@@ -123,7 +132,7 @@ def tile_fp8_extra_decoding_head_d4_kernel(
                 units.append(("w", c, g))
         n_units = len(units)
         wide, bank, grp, codes, planes = {}, {}, {}, {}, {}
-        z, s_t, u_t, hb, hg = {}, {}, {}, {}, {}
+        z, s_t, u_t, hb, hg, h_m = {}, {}, {}, {}, {}, {}
 
         def mode(c, g):
             return MODES.get((c, g), DEFAULT)
@@ -136,16 +145,23 @@ def tile_fp8_extra_decoding_head_d4_kernel(
 
         def widen(i):
             kind, c, g = units[i]
-            w = work.tile([P, NB, 512], BF16, name="wide", align_bytes=64, bufs=4)
+            w = work.tile([P, NB, 512], BF16, name="wide", align_bytes=64, bufs=WB)
             wide[i] = w
             if kind == "w":
                 m = mode(c, g)
                 n_a = m.count("a")
                 assert m[:n_a] == "a" * n_a
-                if n_a < NB:
+                n_e = m.count("e")
+                for a in range(NB - n_e, NB):
+                    for q in range(4):
+                        k0 = 16 * (4 * c + a) + 4 * g + q
+                        nc.scalar.activation(
+                            w[:, a, P * q : P * (q + 1)],
+                            wb[c][:, g, a, P * q : P * (q + 1)].bitcast(FP8), COPY, scale=wsc[:, k0 : k0 + 1])
+                if n_a + n_e < NB:
                     nc.scalar.copy(
-                        w[:, n_a:, :].rearrange("p a k -> p (a k)"),
-                        wb[c][:, g, n_a:, :].rearrange("p a k -> p (a k)").bitcast(FP8),
+                        w[:, n_a : NB - n_e, :].rearrange("p a k -> p (a k)"),
+                        wb[c][:, g, n_a : NB - n_e, :].rearrange("p a k -> p (a k)").bitcast(FP8),
                     )
                 for a in range(n_a):
                     for q in range(4):
@@ -194,19 +210,19 @@ def tile_fp8_extra_decoding_head_d4_kernel(
             if kind == "x":
                 dst = grp[i][:, 1024 * b : 1024 * (b + 1)].bitcast(F32).rearrange("p (a n u) -> p a n u", a=2, u=2)
                 src = bk[:].rearrange("p (a u n) -> p a n u", a=2, u=2)
-                if b == 0:
+                if XEV[b] == "v":
                     nc.vector.tensor_copy(out=dst, in_=src)
                 else:
                     nc.scalar.copy(dst, src)
                 return
             m = mode(c, g)
-            if m[2 * b : 2 * b + 2] in ("aa", "AA"):
+            if m[2 * b : 2 * b + 2] in ("aa", "ae", "ee"):
                 dst = grp[i][:, 1024 * b : 1024 * (b + 1)].bitcast(F32).rearrange("p (a n u) -> p a n u", a=2, u=2)
                 nc.scalar.copy(dst, bk[:].rearrange("p (a u n) -> p a n u", a=2, u=2))
                 return
             for al in range(2):
                 a = 2 * b + al
-                if m[a] == "a":
+                if m[a] in "ae":
                     dst = grp[i][:, 512 * a : 512 * (a + 1)].bitcast(F32).rearrange("p (n u) -> p n u", u=2)
                     nc.scalar.copy(dst, bk[:, 256 * al : 256 * (al + 1)].rearrange("p (u n) -> p n u", u=2))
                     continue
@@ -246,6 +262,11 @@ def tile_fp8_extra_decoding_head_d4_kernel(
         def silu(c, a):
             s = work.tile([P, 4, P], F32, name="s", bufs=6)
             s_t[c, a] = s
+            if HP == "B":
+                nc.scalar.activation(
+                    s[:].rearrange("p t m -> p (t m)").rearrange("p (u j e) -> p u j e", u=2, e=2),
+                    z.pop((c, a))[:].rearrange("p (j u e) -> p u j e", u=2, e=2), SILU)
+                return
             nc.scalar.activation(s[:], z.pop((c, a))[:].rearrange("p (m t) -> p t m", t=4), SILU)
 
         def hadd(c, a):
@@ -253,6 +274,18 @@ def tile_fp8_extra_decoding_head_d4_kernel(
                 return
             u = work.tile([P, 4, P], F32, name="u", bufs=3)
             u_t[c, a] = u
+            if HP == "B":
+                nc.vector.tensor_tensor(
+                    out=u[:].rearrange("p t m -> p (t m)").rearrange("p (u j e) -> p u j e", u=2, e=2),
+                    in0=s_t.pop((c, a))[:].rearrange("p t m -> p (t m)").rearrange("p (u j e) -> p u j e", u=2, e=2),
+                    in1=rt[c][:, a, :].rearrange("p (j u e) -> p u j e", u=2, e=2), op=ADD)
+                hm = work.tile([P, 512], BF16, name="hm", align_bytes=64, bufs=3)
+                h_m[c, a] = hm
+                nc.vector.tensor_tensor(
+                    out=hm[:].rearrange("p (u j e) -> p u j e", u=2, e=2),
+                    in0=u[:].rearrange("p t m -> p (t m)").rearrange("p (u j e) -> p u j e", u=2, e=2),
+                    in1=gb[:, 512 * c : 512 * (c + 1)].rearrange("p (j u e) -> p u j e", u=2, e=2), op=MULT)
+                return
             nc.vector.tensor_tensor(
                 out=u[:], in0=s_t.pop((c, a))[:],
                 in1=rt[c][:, a, :].rearrange("p (m t) -> p t m", t=4), op=ADD,
@@ -261,6 +294,11 @@ def tile_fp8_extra_decoding_head_d4_kernel(
         def htrans(c, a):
             bk = psum.tile([P, 512], F32, name="t", bufs=4)
             hb[c, a] = bk
+            if HP == "B":
+                hm = h_m.pop((c, a))[:].bitcast(F32)
+                for u in range(2):
+                    nc.tensor.transpose(bk[:, P * u : P * (u + 1)], hm[:, P * u : P * (u + 1)], ident[:])
+                return
             if HADD.get((c, a), HDEF) == "p":
                 s = s_t.pop((c, a))
                 for t in range(4):
@@ -275,6 +313,11 @@ def tile_fp8_extra_decoding_head_d4_kernel(
         def hevac(c, a):
             h = work.tile([P, P, 4], BF16, name="hg", align_bytes=64, bufs=3)
             hg[c, a] = h
+            if HP == "B":
+                nc.scalar.copy(
+                    h[:].rearrange("p n t -> p (n t)").bitcast(F32).rearrange("p (n u) -> p n u", u=2),
+                    hb.pop((c, a))[:, :256].rearrange("p (u n) -> p n u", u=2))
+                return
             nc.vector.tensor_tensor(
                 out=h[:], in0=hb.pop((c, a))[:].rearrange("p (t n) -> p n t", t=4),
                 in1=gt[:, c, :].unsqueeze(1).to_broadcast([P, P, 4]), op=MULT,
@@ -309,13 +352,13 @@ def tile_fp8_extra_decoding_head_d4_kernel(
             nc.sync.dma_start(out=out[P * a : P * (a + 1), 512 * v : 512 * (v + 1)], in_=o[:])
 
         ready = []
-        hq = None
+        todo = []
+        prev = None
+        last = NC - 1
         with tc.manual_schedule():
-            widen(0)
-            widen(1)
+            for i in range(LEAD + 1):
+                widen(i)
             for s in range(1, n_units + 3):
-                if s + 1 < n_units:
-                    widen(s + 1)
                 it = s - 1
                 iq = s - 2
                 im = s - 3
@@ -324,26 +367,41 @@ def tile_fp8_extra_decoding_head_d4_kernel(
                     hadd(*h)
                 if 0 <= iq < n_units:
                     quant(iq)
-                if hq:
-                    hquant(*hq)
+                if prev and ORD == 0:
+                    hevac(*prev)
+                if s + LEAD < n_units:
+                    widen(s + LEAD)
+                if prev and ORD == 1:
+                    hevac(*prev)
                 if it < n_units:
                     trans(it, 0)
+                    trans(it, 1)
                     evac(it, 0)
+                if todo and SIL < 4:
+                    for h2 in todo:
+                        silu(*h2)
+                    todo = []
+                if it < n_units:
+                    evac(it, 1)
                 if h:
                     htrans(*h)
-                    hevac(*h)
-                if it < n_units:
-                    trans(it, 1)
-                    evac(it, 1)
-                hq = h
+                if prev:
+                    hquant(*prev)
+                prev = h
                 if im >= 0:
                     mm(im)
                     kind, c, g = units[im]
                     if kind == "w" and g == NG - 1:
                         for a in range(NT):
-                            silu(c, a)
-                            ready.append((c, a))
-            last = NC - 1
+                            if a < SIL or c == last:
+                                silu(c, a)
+                            else:
+                                todo.append((c, a))
+                            if c != last:
+                                ready.append((c, a))
+            if prev:
+                hevac(*prev)
+                hquant(*prev)
 
             def open_group(a, v, tag, cs):
                 if tag == "t":
@@ -354,7 +412,6 @@ def tile_fp8_extra_decoding_head_d4_kernel(
 
             early = range(NC - 1)
             every = range(NC)
-            hquant(*hq)
             hadd(last, 0)
             hadd(last, 1)
             for v in range(NV):

@@ -27,15 +27,24 @@ NT = 4
 NV = 3
 
 X_ON_SCALAR = (3,)
-MODES = {}
-DEFAULT = "aaae"
+MODES = {(c, g): m for c, m in enumerate(("aaae", "aaaa", "aaae", "aaee")) for g in range(4)}
+DEFAULT = "bbbb"
 HADD = {}
 HDEF = "v"
-WB = 4
+WB = 5
 LEAD = 1
 HP = "C"
 XEV = "ss"
-SIL = 4
+STAG = 0
+LQ = 3
+PORD = 2
+PORDS = ("A1Bh2", "ABh12", "12ABh", "hAB12", "12hAB", "AhB12", "12AhB", "A1hB2", "hA1B2")
+EARLY = True
+GB = 3
+VORD = 0
+VORDS = ("aqew", "qaew", "eqaw", "eawq", "awqe", "weaq", "aewq", "qeaw", "eaqw")
+SORT = True
+SPLITMX = True
 ORD = 0
 
 
@@ -49,7 +58,7 @@ def tile_fp8_extra_decoding_head_d4_kernel(
         psum = ctx.enter_context(tc.psum_pool(name="psum", bufs=4))
 
         xs = keep.tile([P, NT, D // P], F32, name="xs")
-        xb = [keep.tile([P, NT, 1024], U8, name="xb%d" % h, align_bytes=64) for h in range(2)]
+        xb = [keep.tile([P, NT, 512], U8, name="xb%d" % g, align_bytes=64) for g in range(NG)]
         wb = [keep.tile([P, NG, NB, 512], U8, name="wb%d" % c, align_bytes=64) for c in range(NC)]
         wsc = keep.tile([P, 256], F32, name="wsc")
         ks = keep.tile([P, 16, NG], F32, name="ks")
@@ -70,12 +79,12 @@ def tile_fp8_extra_decoding_head_d4_kernel(
         nc.vector.tensor_copy(out=identb[:], in_=ident[:])
         nc.gpsimd.memset(psc[:].rearrange("p g n -> p (g n)").bitcast(I32), 0)
 
-        nc.sync.dma_start(out=xs[:], in_=X_scale.rearrange("(a p) j -> p a j", p=P))
+        nc.scalar.dma_start(out=xs[:], in_=X_scale.rearrange("(a p) j -> p a j", p=P))
 
-        def load_x(h):
+        def load_x(g):
             nc.sync.dma_start(
-                out=xb[h][:],
-                in_=X_bytes[:, 1024 * h : 1024 * (h + 1)].rearrange("(a p) k -> p a k", p=P),
+                out=xb[g][:],
+                in_=X_bytes[:, 512 * g : 512 * (g + 1)].rearrange("(a p) k -> p a k", p=P),
             )
 
         def load_w(c, g0, g1):
@@ -93,10 +102,9 @@ def tile_fp8_extra_decoding_head_d4_kernel(
 
         nc.scalar.dma_start(out=wsc[:], in_=W_scale.rearrange("i j -> (i j)").partition_broadcast(P))
         nc.scalar.dma_start(out=gt[:], in_=gain.rearrange("(c p t) -> p c t", p=P, t=4))
-        load_x(0)
-        load_w(0, 0, 2)
-        load_x(1)
-        load_w(0, 2, 4)
+        for g in range(NG):
+            load_x(g)
+            load_w(0, g, g + 1)
         load_w(1, 0, 4)
         load_r(0)
         load_w(2, 0, 4)
@@ -172,10 +180,9 @@ def tile_fp8_extra_decoding_head_d4_kernel(
                             scalar1=wsc[:, k0 : k0 + 1], scalar2=None, op0=MULT,
                         )
                 return
-            h, off = g // 2, 512 * (g % 2)
             for a in range(NT):
                 for q in range(4):
-                    src = xb[h][:, a, off + P * q : off + P * (q + 1)].bitcast(FP8)
+                    src = xb[g][:, a, P * q : P * (q + 1)].bitcast(FP8)
                     scale = xs[:, a, 4 * g + q : 4 * g + q + 1]
                     if permuted(i, a):
                         dst = w[:, a, :].rearrange("p (u j e) -> p j u e", u=2, e=2)[:, 32 * q : 32 * q + 32, :, :]
@@ -205,7 +212,7 @@ def tile_fp8_extra_decoding_head_d4_kernel(
         def evac(i, b):
             kind, c, g = units[i]
             if b == 0:
-                grp[i] = work.tile([P, 2048], BF16, name="grp", align_bytes=64, bufs=3)
+                grp[i] = work.tile([P, 2048], BF16, name="grp", align_bytes=64, bufs=GB)
             bk = bank.pop((i, b))
             if kind == "x":
                 dst = grp[i][:, 1024 * b : 1024 * (b + 1)].bitcast(F32).rearrange("p (a n u) -> p a n u", a=2, u=2)
@@ -239,25 +246,49 @@ def tile_fp8_extra_decoding_head_d4_kernel(
             if kind == "x":
                 cd, pl = xc[g], xp[g]
             else:
-                cd = work.tile([P, 512], U32, name="wcodes", align_bytes=64, bufs=3)
-                pl = work.tile([P, 512], U8, name="wplane", align_bytes=64, bufs=3)
+                cd = work.tile([P, 512], U32, name="wcodes", align_bytes=64, bufs=8)
+                pl = work.tile([P, 512], U8, name="wplane", align_bytes=64, bufs=8)
             codes[i], planes[i] = cd, pl
             nc.vector.quantize_mx(out=cd[:].bitcast(FP8X4), scales=pl[:], in_=grp.pop(i)[:])
 
-        def mm(i):
+        w_unit = {}
+        for i, (kind, c, g) in enumerate(units):
+            if kind == "w":
+                w_unit[c, g] = i
+
+        def one_pass(c, g, a):
+            if g == 0:
+                z[c, a] = psum.tile([P, 512], F32, name="z", bufs=4)
+            i = w_unit[c, g]
+            cols = slice(P * a, P * (a + 1))
+            nc.tensor.matmul_mx(
+                out=z[c, a][:],
+                lhsT=xc[g][:, cols].bitcast(FP8X4), lhsT_scale=xp[g][:, cols],
+                rhs=codes[i][:].bitcast(FP8X4), rhs_scale=planes[i][:],
+                start=(g == 0), stop=(g == NG - 1),
+            )
+
+        nxt = [0] * NT
+
+        def lag(a, w):
+            return a * STAG if w < 12 else min(a * STAG, 15 - w)
+
+        def passes(i):
             kind, c, g = units[i]
             if kind == "x":
-                return
+                return []
+            w = 4 * c + g
+            todo = []
             for a in range(NT):
-                if g == 0:
-                    z[c, a] = psum.tile([P, 512], F32, name="z", bufs=4)
-                cols = slice(P * a, P * (a + 1))
-                nc.tensor.matmul_mx(
-                    out=z[c, a][:],
-                    lhsT=xc[g][:, cols].bitcast(FP8X4), lhsT_scale=xp[g][:, cols],
-                    rhs=codes[i][:].bitcast(FP8X4), rhs_scale=planes[i][:],
-                    start=(g == 0), stop=(g == NG - 1),
-                )
+                while nxt[a] <= w - lag(a, w):
+                    todo.append((nxt[a] // 4, nxt[a] % 4, a))
+                    nxt[a] += 1
+            if SORT:
+                first = {}
+                for c, g, a in todo:
+                    first.setdefault(a, (g == 0 and c > 0, g != NG - 1))
+                todo.sort(key=lambda q: first[q[2]])
+            return todo
 
         def silu(c, a):
             s = work.tile([P, 4, P], F32, name="s", bufs=6)
@@ -292,7 +323,7 @@ def tile_fp8_extra_decoding_head_d4_kernel(
             )
 
         def htrans(c, a):
-            bk = psum.tile([P, 512], F32, name="t", bufs=4)
+            bk = psum.tile([P, 512], F32, name="z" if c == NC - 1 and a % 2 else "t", bufs=4)
             hb[c, a] = bk
             if HP == "B":
                 hm = h_m.pop((c, a))[:].bitcast(F32)
@@ -356,53 +387,6 @@ def tile_fp8_extra_decoding_head_d4_kernel(
         prev = None
         last = NC - 1
         with tc.manual_schedule():
-            for i in range(LEAD + 1):
-                widen(i)
-            for s in range(1, n_units + 3):
-                it = s - 1
-                iq = s - 2
-                im = s - 3
-                h = ready.pop(0) if ready else None
-                if h:
-                    hadd(*h)
-                if 0 <= iq < n_units:
-                    quant(iq)
-                if prev and ORD == 0:
-                    hevac(*prev)
-                if s + LEAD < n_units:
-                    widen(s + LEAD)
-                if prev and ORD == 1:
-                    hevac(*prev)
-                if it < n_units:
-                    trans(it, 0)
-                    trans(it, 1)
-                    evac(it, 0)
-                if todo and SIL < 4:
-                    for h2 in todo:
-                        silu(*h2)
-                    todo = []
-                if it < n_units:
-                    evac(it, 1)
-                if h:
-                    htrans(*h)
-                if prev:
-                    hquant(*prev)
-                prev = h
-                if im >= 0:
-                    mm(im)
-                    kind, c, g = units[im]
-                    if kind == "w" and g == NG - 1:
-                        for a in range(NT):
-                            if a < SIL or c == last:
-                                silu(c, a)
-                            else:
-                                todo.append((c, a))
-                            if c != last:
-                                ready.append((c, a))
-            if prev:
-                hevac(*prev)
-                hquant(*prev)
-
             def open_group(a, v, tag, cs):
                 if tag == "t":
                     acc[a, v] = psum.tile([P, 512], F32, name="t", bufs=4)
@@ -412,35 +396,90 @@ def tile_fp8_extra_decoding_head_d4_kernel(
 
             early = range(NC - 1)
             every = range(NC)
+            opened = 0
+            for i in range(LEAD + 1):
+                widen(i)
+            for s in range(1, n_units + LQ + 1):
+                it = s - 1
+                iq = s - LQ
+                im = s - LQ - 1
+                ps = passes(im) if im >= 0 else []
+                n1 = len(ps) // 2 if SPLITMX else 0
+
+                def run(some):
+                    for c, g, a in some:
+                        one_pass(c, g, a)
+                        if g == NG - 1:
+                            silu(c, a)
+                            if c != last:
+                                ready.append((c, a))
+
+                h = ready.pop(0) if ready else None
+                for what in VORDS[VORD]:
+                    if what == "a" and h:
+                        hadd(*h)
+                    if what == "q" and 0 <= iq < n_units:
+                        quant(iq)
+                    if what == "e" and prev:
+                        hevac(*prev)
+                    if what == "w" and s + LEAD < n_units:
+                        widen(s + LEAD)
+                for what in PORDS[PORD]:
+                    if what in "AB" and it < n_units:
+                        trans(it, "AB".index(what))
+                        evac(it, "AB".index(what))
+                    if what == "1":
+                        run(ps[:n1])
+                    if what == "2":
+                        run(ps[n1:])
+                    if what == "h" and h:
+                        htrans(*h)
+                if prev:
+                    hquant(*prev)
+                prev = h
+                if EARLY and it >= n_units and opened < NV:
+                    open_group(0, opened, "t", early)
+                    opened += 1
+            while prev or ready:
+                if prev:
+                    hevac(*prev)
+                h = ready.pop(0) if ready else None
+                if h:
+                    hadd(*h)
+                    htrans(*h)
+                if prev:
+                    hquant(*prev)
+                prev = h
+
             hadd(last, 0)
             hadd(last, 1)
-            for v in range(NV):
+            for v in range(opened, NV):
                 open_group(0, v, "t", early)
+            open_group(1, 0, "z", early)
             htrans(last, 0)
+            htrans(last, 1)
             hevac(last, 0)
+            hevac(last, 1)
             hadd(last, 2)
             hquant(last, 0)
-            for v in range(NV):
-                open_group(1, v, "z", early)
-            htrans(last, 1)
-            hevac(last, 1)
-            hadd(last, 3)
             hquant(last, 1)
+            hadd(last, 3)
+            for v in range(1, NV):
+                open_group(1, v, "z", early)
             for v in range(NV):
                 logits(0, v, [last])
                 store(0, v)
             htrans(last, 2)
+            htrans(last, 3)
             hevac(last, 2)
+            hevac(last, 3)
             for v in range(NV):
                 logits(1, v, [last])
                 store(1, v)
             hquant(last, 2)
-            htrans(last, 3)
-            hevac(last, 3)
+            hquant(last, 3)
             for v in range(NV):
                 open_group(2, v, "t" if v < 2 else "z", every)
-                if v == 0:
-                    hquant(last, 3)
                 store(2, v)
             for v in range(NV - 1):
                 open_group(3, v, "z" if v == 0 else "t", every)

@@ -26,16 +26,18 @@ NC = 4
 NT = 4
 NV = 3
 
-X_ON_SCALAR = (3,)
-MODES = {(c, g): m for c, m in enumerate(("aaae", "aaaa", "aaae", "aaee")) for g in range(4)}
-DEFAULT = "bbbb"
+XSG = ((2, 3), (3,), (2, 3), (3,))
+SQ = {(c, g): (3,) for c in range(1, 4) for g in (1, 2)}
+SDEF = ()
 HADD = {}
 HDEF = "v"
 WB = 5
 LEAD = 1
 HP = "C"
 XEV = "ss"
-STAG = 0
+WEV = {}
+WQ = 7
+LAGS = (0, 0, 0, 0)
 LQ = 3
 PORD = 2
 PORDS = ("A1Bh2", "ABh12", "12ABh", "hAB12", "12hAB", "AhB12", "12AhB", "A1hB2", "hA1B2")
@@ -59,9 +61,9 @@ def tile_fp8_extra_decoding_head_d4_kernel(
 
         xs = keep.tile([P, NT, D // P], F32, name="xs")
         xb = [keep.tile([P, NT, 512], U8, name="xb%d" % g, align_bytes=64) for g in range(NG)]
-        wb = [keep.tile([P, NG, NB, 512], U8, name="wb%d" % c, align_bytes=64) for c in range(NC)]
+        wb = [keep.tile([P, NG, 4, NB, P], U8, name="wb%d" % c, align_bytes=64) for c in range(NC)]
         wsc = keep.tile([P, 256], F32, name="wsc")
-        ks = keep.tile([P, 16, NG], F32, name="ks")
+        wsk = keep.tile([P, NC, 16], F32, name="wsk")
         gt = keep.tile([P, NC, 4], BF16, name="gt")
         rt = [keep.tile([P, NT, 512], BF16, name="rt%d" % c, align_bytes=64) for c in range(NC)]
         pw = keep.tile([P, NG, 2 * V], U8, name="pw", align_bytes=64)
@@ -89,10 +91,12 @@ def tile_fp8_extra_decoding_head_d4_kernel(
 
         def load_w(c, g0, g1):
             for g in range(g0, g1):
-                nc.sync.dma_start(
-                    out=wb[c][:, g, :, :],
-                    in_=W_bytes[512 * c : 512 * (c + 1), 512 * g : 512 * (g + 1)].rearrange("(a p) k -> p a k", p=P),
-                )
+                for q in range(4):
+                    k0 = 512 * g + P * q
+                    nc.sync.dma_start(
+                        out=wb[c][:, g, q, :, :],
+                        in_=W_bytes[512 * c : 512 * (c + 1), k0 : k0 + P].rearrange("(p j) k -> p j k", j=4),
+                    )
 
         def load_r(c):
             nc.sync.dma_start(
@@ -122,8 +126,8 @@ def tile_fp8_extra_decoding_head_d4_kernel(
         for q in range(4):
             rows = slice(32 * q, 32 * q + 32)
             nc.vector.tensor_copy(
-                out=ks[rows, :, :],
-                in_=wsc[rows, :].rearrange("p (i g r) -> p i g r", i=16, g=NG)[:, :, :, q],
+                out=wsk[rows, :, :],
+                in_=wsc[rows, :].rearrange("p (c i k) -> p c i k", i=4, k=16)[:, :, q, :],
             )
 
         xc = [keep.tile([P, 512], U32, name="xc%d" % g, align_bytes=64) for g in range(NG)]
@@ -142,43 +146,28 @@ def tile_fp8_extra_decoding_head_d4_kernel(
         wide, bank, grp, codes, planes = {}, {}, {}, {}, {}
         z, s_t, u_t, hb, hg, h_m = {}, {}, {}, {}, {}, {}
 
-        def mode(c, g):
-            return MODES.get((c, g), DEFAULT)
-
         def permuted(i, a):
             kind, c, g = units[i]
             if kind == "x":
-                return a not in X_ON_SCALAR
-            return mode(c, g)[a] == "a"
+                return a not in XSG[g]
+            return False
 
         def widen(i):
             kind, c, g = units[i]
             w = work.tile([P, NB, 512], BF16, name="wide", align_bytes=64, bufs=WB)
             wide[i] = w
             if kind == "w":
-                m = mode(c, g)
-                n_a = m.count("a")
-                assert m[:n_a] == "a" * n_a
-                n_e = m.count("e")
-                for a in range(NB - n_e, NB):
-                    for q in range(4):
-                        k0 = 16 * (4 * c + a) + 4 * g + q
-                        nc.scalar.activation(
-                            w[:, a, P * q : P * (q + 1)],
-                            wb[c][:, g, a, P * q : P * (q + 1)].bitcast(FP8), COPY, scale=wsc[:, k0 : k0 + 1])
-                if n_a + n_e < NB:
-                    nc.scalar.copy(
-                        w[:, n_a : NB - n_e, :].rearrange("p a k -> p (a k)"),
-                        wb[c][:, g, n_a : NB - n_e, :].rearrange("p a k -> p (a k)").bitcast(FP8),
-                    )
-                for a in range(n_a):
-                    for q in range(4):
-                        k0 = 16 * (4 * c + a) + 4 * g + q
+                on_scalar = SQ.get((c, g), SDEF)
+                for q in range(4):
+                    scale = wsk[:, c, 4 * g + q : 4 * g + q + 1]
+                    if q in on_scalar:
+                        for j in range(4):
+                            nc.scalar.activation(
+                                w[:, j, P * q : P * (q + 1)], wb[c][:, g, q, j, :].bitcast(FP8), COPY, scale=scale)
+                    else:
                         nc.vector.tensor_scalar(
-                            out=w[:, a, :].rearrange("p (u j e) -> p j u e", u=2, e=2)[:, 32 * q : 32 * q + 32, :, :],
-                            in0=wb[c][:, g, a, P * q : P * (q + 1)].bitcast(FP8).rearrange("p (j u e) -> p j u e", u=2, e=2),
-                            scalar1=wsc[:, k0 : k0 + 1], scalar2=None, op0=MULT,
-                        )
+                            out=w[:, :, P * q : P * (q + 1)], in0=wb[c][:, g, q, :, :].bitcast(FP8),
+                            scalar1=scale, scalar2=None, op0=MULT)
                 return
             for a in range(NT):
                 for q in range(4):
@@ -214,32 +203,13 @@ def tile_fp8_extra_decoding_head_d4_kernel(
             if b == 0:
                 grp[i] = work.tile([P, 2048], BF16, name="grp", align_bytes=64, bufs=GB)
             bk = bank.pop((i, b))
-            if kind == "x":
-                dst = grp[i][:, 1024 * b : 1024 * (b + 1)].bitcast(F32).rearrange("p (a n u) -> p a n u", a=2, u=2)
-                src = bk[:].rearrange("p (a u n) -> p a n u", a=2, u=2)
-                if XEV[b] == "v":
-                    nc.vector.tensor_copy(out=dst, in_=src)
-                else:
-                    nc.scalar.copy(dst, src)
-                return
-            m = mode(c, g)
-            if m[2 * b : 2 * b + 2] in ("aa", "ae", "ee"):
-                dst = grp[i][:, 1024 * b : 1024 * (b + 1)].bitcast(F32).rearrange("p (a n u) -> p a n u", a=2, u=2)
-                nc.scalar.copy(dst, bk[:].rearrange("p (a u n) -> p a n u", a=2, u=2))
-                return
-            for al in range(2):
-                a = 2 * b + al
-                if m[a] in "ae":
-                    dst = grp[i][:, 512 * a : 512 * (a + 1)].bitcast(F32).rearrange("p (n u) -> p n u", u=2)
-                    nc.scalar.copy(dst, bk[:, 256 * al : 256 * (al + 1)].rearrange("p (u n) -> p n u", u=2))
-                    continue
-                dst = grp[i][:, 512 * a : 512 * (a + 1)].rearrange("p (n u e) -> p n u e", u=2, e=2)
-                src = bk[:, 256 * al : 256 * (al + 1)].bitcast(BF16).rearrange("p (u n e) -> p n u e", u=2, e=2)
-                scale = ks[:, 4 * c + a, g : g + 1]
-                if m[a] == "c":
-                    nc.scalar.activation(dst, src, COPY, scale=scale)
-                else:
-                    nc.vector.tensor_scalar(out=dst, in0=src, scalar1=scale, scalar2=None, op0=MULT)
+            dst = grp[i][:, 1024 * b : 1024 * (b + 1)].bitcast(F32).rearrange("p (a n u) -> p a n u", a=2, u=2)
+            src = bk[:].rearrange("p (a u n) -> p a n u", a=2, u=2)
+            who = XEV[b] if kind == "x" else WEV.get((c, g), "ss")[b]
+            if who == "v":
+                nc.vector.tensor_copy(out=dst, in_=src)
+            else:
+                nc.scalar.copy(dst, src)
 
         def quant(i):
             kind, c, g = units[i]
@@ -271,7 +241,7 @@ def tile_fp8_extra_decoding_head_d4_kernel(
         nxt = [0] * NT
 
         def lag(a, w):
-            return a * STAG if w < 12 else min(a * STAG, 15 - w)
+            return LAGS[a] if w < 12 else min(LAGS[a], 15 - w)
 
         def passes(i):
             kind, c, g = units[i]
@@ -298,7 +268,7 @@ def tile_fp8_extra_decoding_head_d4_kernel(
                     s[:].rearrange("p t m -> p (t m)").rearrange("p (u j e) -> p u j e", u=2, e=2),
                     z.pop((c, a))[:].rearrange("p (j u e) -> p u j e", u=2, e=2), SILU)
                 return
-            nc.scalar.activation(s[:], z.pop((c, a))[:].rearrange("p (m t) -> p t m", t=4), SILU)
+            nc.scalar.activation(s[:].rearrange("p t m -> p (t m)"), z.pop((c, a))[:], SILU)
 
         def hadd(c, a):
             if HADD.get((c, a), HDEF) == "p":

from contextlib import ExitStack

import concourse.mybir as mybir
from concourse.masks import make_identity

T, D, V = 512, 2048, 1536
P = 128
FLOPS = 2 * T * D * (D + V)

F32 = mybir.dt.float32
BF16 = mybir.dt.bfloat16
U32 = mybir.dt.uint32
I32 = mybir.dt.int32
U8 = mybir.dt.uint8
FP8 = mybir.dt.float8_e4m3fn
FP8X4 = mybir.dt.float8_e4m3fn_x4
FP4X4 = mybir.dt.float4_e2m1fn_x4
COPY = mybir.ActivationFunctionType.Copy
SILU = mybir.ActivationFunctionType.Silu
MULT = mybir.AluOpType.mult
ADD = mybir.AluOpType.add

NB = 4
NG = 4
NC = 4
NT = 4
NV = 3

XSG = ((2, 3), (3,), (2, 3), (3,))
SQ = {(c, g): (3,) for c in range(1, 4) for g in (1, 2)}
SDEF = ()
HADD = {}
HDEF = "v"
WB = 5
LEAD = 1
HP = "C"
XEV = "ss"
WEV = {}
WQ = 7
LAGS = (0, 0, 0, 0)
LQ = 3
PORD = 2
PORDS = ("A1Bh2", "ABh12", "12ABh", "hAB12", "12hAB", "AhB12", "12AhB", "A1hB2", "hA1B2")
EARLY = True
GB = 3
VORD = 0
VORDS = ("aqew", "qaew", "eqaw", "eawq", "awqe", "weaq", "aewq", "qeaw", "eaqw")
SORT = True
SPLITMX = True
ORD = 0


def tile_fp8_extra_decoding_head_d4_kernel(
    tc, X_bytes, X_scale, W_bytes, W_scale, resid, gain, P_words, P_scales, out
):
    nc = tc.nc
    with ExitStack() as ctx:
        keep = ctx.enter_context(tc.tile_pool(name="keep", bufs=1))
        work = ctx.enter_context(tc.tile_pool(name="work", bufs=3))
        psum = ctx.enter_context(tc.psum_pool(name="psum", bufs=4))

        xs = keep.tile([P, NT, D // P], F32, name="xs")
        xb = [keep.tile([P, NT, 512], U8, name="xb%d" % g, align_bytes=64) for g in range(NG)]
        wb = [keep.tile([P, NG, 4, NB, P], U8, name="wb%d" % c, align_bytes=64) for c in range(NC)]
        wsc = keep.tile([P, 256], F32, name="wsc")
        wsk = keep.tile([P, NC, 16], F32, name="wsk")
        gt = keep.tile([P, NC, 4], BF16, name="gt")
        rt = [keep.tile([P, NT, 512], BF16, name="rt%d" % c, align_bytes=64) for c in range(NC)]
        pw = keep.tile([P, NG, 2 * V], U8, name="pw", align_bytes=64)
        psc = keep.tile([P, NG, V], U8, name="psc", align_bytes=64)
        ident = keep.tile([P, P], F32, name="ident")
        warm = keep.tile([P, 1], F32, name="warm")

        nc.gpsimd.memset(warm[:], 0.0)
        nc.scalar.activation(warm[:], warm[:], SILU)
        make_identity(nc, ident[:])
        if HP == "B":
            gb = keep.tile([P, D], BF16, name="gb")
            nc.scalar.dma_start(out=gb[:], in_=gain.partition_broadcast(P))
        identb = keep.tile([P, P], BF16, name="identb")
        nc.vector.tensor_copy(out=identb[:], in_=ident[:])
        nc.gpsimd.memset(psc[:].rearrange("p g n -> p (g n)").bitcast(I32), 0)

        nc.scalar.dma_start(out=xs[:], in_=X_scale.rearrange("(a p) j -> p a j", p=P))

        def load_x(g):
            nc.sync.dma_start(
                out=xb[g][:],
                in_=X_bytes[:, 512 * g : 512 * (g + 1)].rearrange("(a p) k -> p a k", p=P),
            )

        def load_w(c, g0, g1):
            for g in range(g0, g1):
                for q in range(4):
                    k0 = 512 * g + P * q
                    nc.sync.dma_start(
                        out=wb[c][:, g, q, :, :],
                        in_=W_bytes[512 * c : 512 * (c + 1), k0 : k0 + P].rearrange("(p j) k -> p j k", j=4),
                    )

        def load_r(c):
            nc.sync.dma_start(
                out=rt[c][:],
                in_=resid[:, 512 * c : 512 * (c + 1)].rearrange("(a p) k -> p a k", p=P),
            )

        nc.scalar.dma_start(out=wsc[:], in_=W_scale.rearrange("i j -> (i j)").partition_broadcast(P))
        nc.scalar.dma_start(out=gt[:], in_=gain.rearrange("(c p t) -> p c t", p=P, t=4))
        for g in range(NG):
            load_x(g)
            load_w(0, g, g + 1)
        load_w(1, 0, 4)
        load_r(0)
        load_w(2, 0, 4)
        load_r(1)
        load_w(3, 0, 4)
        for q in range(4):
            nc.sync.dma_start(
                out=psc[32 * q : 32 * q + 4, :, :].rearrange("p g n -> p (g n)").bitcast(I32).rearrange("p (g n) -> p g n", g=NG),
                in_=P_scales[:, 4 * q : 4 * q + 4, :].bitcast(I32).rearrange("g r n -> r g n"),
            )
        nc.sync.dma_start(out=pw[:], in_=P_words.rearrange("g p n -> p g n"))
        load_r(2)
        load_r(3)

        for q in range(4):
            rows = slice(32 * q, 32 * q + 32)
            nc.vector.tensor_copy(
                out=wsk[rows, :, :],
                in_=wsc[rows, :].rearrange("p (c i k) -> p c i k", i=4, k=16)[:, :, q, :],
            )

        xc = [keep.tile([P, 512], U32, name="xc%d" % g, align_bytes=64) for g in range(NG)]
        xp = [keep.tile([P, 512], U8, name="xp%d" % g, align_bytes=64) for g in range(NG)]
        hc = [keep.tile([P, 512], U32, name="hc%d" % c, align_bytes=64) for c in range(NC)]
        hp = [keep.tile([P, 512], U8, name="hp%d" % c, align_bytes=64) for c in range(NC)]

        units = []
        for g in range(NG):
            units.append(("x", 0, g))
            units.append(("w", 0, g))
        for c in range(1, NC):
            for g in range(NG):
                units.append(("w", c, g))
        n_units = len(units)
        wide, bank, grp, codes, planes = {}, {}, {}, {}, {}
        z, s_t, u_t, hb, hg, h_m = {}, {}, {}, {}, {}, {}

        def permuted(i, a):
            kind, c, g = units[i]
            if kind == "x":
                return a not in XSG[g]
            return False

        def widen(i):
            kind, c, g = units[i]
            w = work.tile([P, NB, 512], BF16, name="wide", align_bytes=64, bufs=WB)
            wide[i] = w
            if kind == "w":
                on_scalar = SQ.get((c, g), SDEF)
                for q in range(4):
                    scale = wsk[:, c, 4 * g + q : 4 * g + q + 1]
                    if q in on_scalar:
                        for j in range(4):
                            nc.scalar.activation(
                                w[:, j, P * q : P * (q + 1)], wb[c][:, g, q, j, :].bitcast(FP8), COPY, scale=scale)
                    else:
                        nc.vector.tensor_scalar(
                            out=w[:, :, P * q : P * (q + 1)], in0=wb[c][:, g, q, :, :].bitcast(FP8),
                            scalar1=scale, scalar2=None, op0=MULT)
                return
            for a in range(NT):
                for q in range(4):
                    src = xb[g][:, a, P * q : P * (q + 1)].bitcast(FP8)
                    scale = xs[:, a, 4 * g + q : 4 * g + q + 1]
                    if permuted(i, a):
                        dst = w[:, a, :].rearrange("p (u j e) -> p j u e", u=2, e=2)[:, 32 * q : 32 * q + 32, :, :]
                        nc.vector.tensor_scalar(
                            out=dst,
                            in0=src.rearrange("p (j u e) -> p j u e", u=2, e=2),
                            scalar1=scale, scalar2=None, op0=MULT,
                        )
                    else:
                        nc.scalar.activation(w[:, a, P * q : P * (q + 1)], src, COPY, scale=scale)

        def trans(i, b):
            kind, c, g = units[i]
            bk = psum.tile([P, 512], F32, name="t", bufs=4)
            bank[i, b] = bk
            dst = bk[:].rearrange("p (a u n) -> p a u n", a=2, u=2)
            words = wide[i][:].rearrange("p a k -> p (a k)").bitcast(F32)
            for al in range(2):
                a = 2 * b + al
                for u in range(2):
                    if permuted(i, a):
                        src = words[:, 256 * a + 128 * u : 256 * a + 128 * (u + 1)]
                    else:
                        src = words[:, 256 * a + u : 256 * (a + 1) : 2]
                    nc.tensor.transpose(dst[:, al, u, :], src, ident[:])

        def evac(i, b):
            kind, c, g = units[i]
            if b == 0:
                grp[i] = work.tile([P, 2048], BF16, name="grp", align_bytes=64, bufs=GB)
            bk = bank.pop((i, b))
            dst = grp[i][:, 1024 * b : 1024 * (b + 1)].bitcast(F32).rearrange("p (a n u) -> p a n u", a=2, u=2)
            src = bk[:].rearrange("p (a u n) -> p a n u", a=2, u=2)
            who = XEV[b] if kind == "x" else WEV.get((c, g), "ss")[b]
            if who == "v":
                nc.vector.tensor_copy(out=dst, in_=src)
            else:
                nc.scalar.copy(dst, src)

        def quant(i):
            kind, c, g = units[i]
            if kind == "x":
                cd, pl = xc[g], xp[g]
            else:
                cd = work.tile([P, 512], U32, name="wcodes", align_bytes=64, bufs=8)
                pl = work.tile([P, 512], U8, name="wplane", align_bytes=64, bufs=8)
            codes[i], planes[i] = cd, pl
            nc.vector.quantize_mx(out=cd[:].bitcast(FP8X4), scales=pl[:], in_=grp.pop(i)[:])

        w_unit = {}
        for i, (kind, c, g) in enumerate(units):
            if kind == "w":
                w_unit[c, g] = i

        def one_pass(c, g, a):
            if g == 0:
                z[c, a] = psum.tile([P, 512], F32, name="z", bufs=4)
            i = w_unit[c, g]
            cols = slice(P * a, P * (a + 1))
            nc.tensor.matmul_mx(
                out=z[c, a][:],
                lhsT=xc[g][:, cols].bitcast(FP8X4), lhsT_scale=xp[g][:, cols],
                rhs=codes[i][:].bitcast(FP8X4), rhs_scale=planes[i][:],
                start=(g == 0), stop=(g == NG - 1),
            )

        nxt = [0] * NT

        def lag(a, w):
            return LAGS[a] if w < 12 else min(LAGS[a], 15 - w)

        def passes(i):
            kind, c, g = units[i]
            if kind == "x":
                return []
            w = 4 * c + g
            todo = []
            for a in range(NT):
                while nxt[a] <= w - lag(a, w):
                    todo.append((nxt[a] // 4, nxt[a] % 4, a))
                    nxt[a] += 1
            if SORT:
                first = {}
                for c, g, a in todo:
                    first.setdefault(a, (g == 0 and c > 0, g != NG - 1))
                todo.sort(key=lambda q: first[q[2]])
            return todo

        def silu(c, a):
            s = work.tile([P, 4, P], F32, name="s", bufs=6)
            s_t[c, a] = s
            if HP == "B":
                nc.scalar.activation(
                    s[:].rearrange("p t m -> p (t m)").rearrange("p (u j e) -> p u j e", u=2, e=2),
                    z.pop((c, a))[:].rearrange("p (j u e) -> p u j e", u=2, e=2), SILU)
                return
            nc.scalar.activation(s[:].rearrange("p t m -> p (t m)"), z.pop((c, a))[:], SILU)

        def hadd(c, a):
            if HADD.get((c, a), HDEF) == "p":
                return
            u = work.tile([P, 4, P], F32, name="u", bufs=3)
            u_t[c, a] = u
            if HP == "B":
                nc.vector.tensor_tensor(
                    out=u[:].rearrange("p t m -> p (t m)").rearrange("p (u j e) -> p u j e", u=2, e=2),
                    in0=s_t.pop((c, a))[:].rearrange("p t m -> p (t m)").rearrange("p (u j e) -> p u j e", u=2, e=2),
                    in1=rt[c][:, a, :].rearrange("p (j u e) -> p u j e", u=2, e=2), op=ADD)
                hm = work.tile([P, 512], BF16, name="hm", align_bytes=64, bufs=3)
                h_m[c, a] = hm
                nc.vector.tensor_tensor(
                    out=hm[:].rearrange("p (u j e) -> p u j e", u=2, e=2),
                    in0=u[:].rearrange("p t m -> p (t m)").rearrange("p (u j e) -> p u j e", u=2, e=2),
                    in1=gb[:, 512 * c : 512 * (c + 1)].rearrange("p (j u e) -> p u j e", u=2, e=2), op=MULT)
                return
            nc.vector.tensor_tensor(
                out=u[:], in0=s_t.pop((c, a))[:],
                in1=rt[c][:, a, :].rearrange("p (m t) -> p t m", t=4), op=ADD,
            )

        def htrans(c, a):
            bk = psum.tile([P, 512], F32, name="z" if c == NC - 1 and a % 2 else "t", bufs=4)
            hb[c, a] = bk
            if HP == "B":
                hm = h_m.pop((c, a))[:].bitcast(F32)
                for u in range(2):
                    nc.tensor.transpose(bk[:, P * u : P * (u + 1)], hm[:, P * u : P * (u + 1)], ident[:])
                return
            if HADD.get((c, a), HDEF) == "p":
                s = s_t.pop((c, a))
                for t in range(4):
                    o = bk[:, P * t : P * (t + 1)]
                    nc.tensor.matmul(o, lhsT=rt[c][:, a, t : 512 : 4], rhs=identb[:], start=True, stop=False)
                    nc.tensor.matmul(o, lhsT=s[:, t, :], rhs=ident[:], start=False, stop=True, is_transpose=True)
                return
            u = u_t.pop((c, a))
            for t in range(4):
                nc.tensor.transpose(bk[:, P * t : P * (t + 1)], u[:, t, :], ident[:])

        def hevac(c, a):
            h = work.tile([P, P, 4], BF16, name="hg", align_bytes=64, bufs=3)
            hg[c, a] = h
            if HP == "B":
                nc.scalar.copy(
                    h[:].rearrange("p n t -> p (n t)").bitcast(F32).rearrange("p (n u) -> p n u", u=2),
                    hb.pop((c, a))[:, :256].rearrange("p (u n) -> p n u", u=2))
                return
            nc.vector.tensor_tensor(
                out=h[:], in0=hb.pop((c, a))[:].rearrange("p (t n) -> p n t", t=4),
                in1=gt[:, c, :].unsqueeze(1).to_broadcast([P, P, 4]), op=MULT,
            )

        def hquant(c, a):
            cols = slice(P * a, P * (a + 1))
            nc.vector.quantize_mx(
                out=hc[c][:, cols].bitcast(FP8X4), scales=hp[c][:, cols],
                in_=hg.pop((c, a))[:].rearrange("p n t -> p (n t)"),
            )

        acc = {}

        def logits(a, v, cs):
            for c in cs:
                cols = slice(P * a, P * (a + 1))
                nc.tensor.matmul_mx(
                    out=acc[a, v][:],
                    lhsT=hc[c][:, cols].bitcast(FP8X4), lhsT_scale=hp[c][:, cols],
                    rhs=pw[:, c, 1024 * v : 1024 * (v + 1)].bitcast(FP4X4),
                    rhs_scale=psc[:, c, 512 * v : 512 * (v + 1)],
                    start=(c == 0), stop=(c == NC - 1),
                )

        def store(a, v):
            o = work.tile([P, 512], F32, name="o", bufs=6)
            if (a * NV + v) % 2:
                nc.scalar.copy(o[:], acc.pop((a, v))[:])
            else:
                nc.vector.tensor_copy(out=o[:], in_=acc.pop((a, v))[:])
            nc.sync.dma_start(out=out[P * a : P * (a + 1), 512 * v : 512 * (v + 1)], in_=o[:])

        ready = []
        todo = []
        prev = None
        last = NC - 1
        with tc.manual_schedule():
            def open_group(a, v, tag, cs):
                if tag == "t":
                    acc[a, v] = psum.tile([P, 512], F32, name="t", bufs=4)
                else:
                    acc[a, v] = psum.tile([P, 512], F32, name="z", bufs=4)
                logits(a, v, cs)

            early = range(NC - 1)
            every = range(NC)
            opened = 0
            for i in range(LEAD + 1):
                widen(i)
            for s in range(1, n_units + LQ + 1):
                it = s - 1
                iq = s - LQ
                im = s - LQ - 1
                ps = passes(im) if im >= 0 else []
                n1 = len(ps) // 2 if SPLITMX else 0

                def run(some):
                    for c, g, a in some:
                        one_pass(c, g, a)
                        if g == NG - 1:
                            silu(c, a)
                            if c != last:
                                ready.append((c, a))

                h = ready.pop(0) if ready else None
                for what in VORDS[VORD]:
                    if what == "a" and h:
                        hadd(*h)
                    if what == "q" and 0 <= iq < n_units:
                        quant(iq)
                    if what == "e" and prev:
                        hevac(*prev)
                    if what == "w" and s + LEAD < n_units:
                        widen(s + LEAD)
                for what in PORDS[PORD]:
                    if what in "AB" and it < n_units:
                        trans(it, "AB".index(what))
                        evac(it, "AB".index(what))
                    if what == "1":
                        run(ps[:n1])
                    if what == "2":
                        run(ps[n1:])
                    if what == "h" and h:
                        htrans(*h)
                if prev:
                    hquant(*prev)
                prev = h
                if EARLY and it >= n_units and opened < NV:
                    open_group(0, opened, "t", early)
                    opened += 1
            while prev or ready:
                if prev:
                    hevac(*prev)
                h = ready.pop(0) if ready else None
                if h:
                    hadd(*h)
                    htrans(*h)
                if prev:
                    hquant(*prev)
                prev = h

            hadd(last, 0)
            hadd(last, 1)
            for v in range(opened, NV):
                open_group(0, v, "t", early)
            open_group(1, 0, "z", early)
            htrans(last, 0)
            htrans(last, 1)
            hevac(last, 0)
            hevac(last, 1)
            hadd(last, 2)
            hquant(last, 0)
            hquant(last, 1)
            hadd(last, 3)
            for v in range(1, NV):
                open_group(1, v, "z", early)
            for v in range(NV):
                logits(0, v, [last])
                store(0, v)
            htrans(last, 2)
            htrans(last, 3)
            hevac(last, 2)
            hevac(last, 3)
            for v in range(NV):
                logits(1, v, [last])
                store(1, v)
            hquant(last, 2)
            hquant(last, 3)
            for v in range(NV):
                open_group(2, v, "t" if v < 2 else "z", every)
                store(2, v)
            for v in range(NV - 1):
                open_group(3, v, "z" if v == 0 else "t", every)
                store(3, v)
            v = NV - 1
            a = NT - 1
            cols = slice(P * a, P * (a + 1))
            for part, (q0, q1) in enumerate(((0, 3), (3, 4))):
                if part:
                    bk = psum.tile([P, 512], F32, name="z", bufs=4)
                else:
                    bk = psum.tile([P, 512], F32, name="t", bufs=4)
                for q in range(q0, q1):
                    n0 = 512 * v + P * q
                    for c in every:
                        nc.tensor.matmul_mx(
                            out=bk[:, P * q : P * (q + 1)],
                            lhsT=hc[c][:, cols].bitcast(FP8X4), lhsT_scale=hp[c][:, cols],
                            rhs=pw[:, c, 2 * n0 : 2 * n0 + 2 * P].bitcast(FP4X4),
                            rhs_scale=psc[:, c, n0 : n0 + P],
                            start=(c == 0), stop=(c == NC - 1),
                        )
                width = P * (q1 - q0)
                o = work.tile([P, 512], F32, name="oh", bufs=2)
                if part:
                    nc.vector.tensor_copy(out=o[:, :width], in_=bk[:, P * q0 : P * q1])
                else:
                    nc.scalar.copy(o[:, :width], bk[:, P * q0 : P * q1])
                n0 = 512 * v + P * q0
                nc.sync.dma_start(out=out[P * a : P * (a + 1), n0 : n0 + width], in_=o[:, :width])
